import numpy as np
import ml_dtypes


def mxq(x, axis, fmt="e4m3"):
    dtype, down = {"e4m3": (ml_dtypes.float8_e4m3fn, 7), "e5m2": (ml_dtypes.float8_e5m2, 14)}[fmt]
    v = np.moveaxis(np.asarray(x, np.float32).astype(ml_dtypes.bfloat16).astype(np.float64), axis, -1)
    blocks = v.reshape(v.shape[:-1] + (-1, 32))
    amax = np.abs(blocks).max(-1, keepdims=True)
    byte = np.maximum(np.where(amax > 0, np.frexp(amax)[1] - 1 + 127, 0) - down, 1)
    scale = np.exp2(byte - 127.0)
    codes = (blocks / scale).astype(np.float32).astype(dtype).astype(np.float64)
    return np.moveaxis((codes * scale).reshape(v.shape), -1, axis)


WIDE = False


def mx_kscale(k):
    if not WIDE:
        return np.ones(k)
    levels = np.array([10, -10, 5, -5, 0])
    if k % 512:
        return np.exp2(np.random.permutation(np.resize(levels, k // 32))).repeat(32)
    a = np.empty((k // 512, 16))
    for p in range(k // 512):
        a[p, :8] = np.random.permutation(np.resize(levels, 8))
        for g in range(8):
            far = levels[np.abs(levels - a[p, g]) >= 10]
            a[p, g + 8] = far[np.random.randint(len(far))]
    return np.exp2(a.ravel()).repeat(32)


def f64(x):
    return np.asarray(x).astype(np.float64)


def striped(idx):
    return np.tile(idx.reshape(-1, 16).T, (8, 1)).astype(np.uint16)


def unstriped(offs):
    return offs[:16].T.reshape(-1).astype(np.int64)


E2M1 = np.array([0.0, 0.5, 1.0, 1.5, 2.0, 3.0, 4.0, 6.0, -0.0, -0.5, -1.0, -1.5, -2.0, -3.0, -4.0, -6.0])


def pack_weight(w, fmt):
    k, n = w.shape
    w = f64(np.asarray(w, np.float32).astype(ml_dtypes.bfloat16)).reshape(k // 32, 32, n)
    amax = np.abs(w).max(1)
    if fmt == "e4m3":
        byte = np.frexp(amax)[1] - 1 + 127 - 7
    else:
        mant, ex = np.frexp(amax / 6.0)
        byte = np.where(mant > 0.5, ex, ex - 1) + 127
    byte = np.clip(np.where(amax > 0, byte, 1), 1, 254)
    scaled = (w * np.exp2(127.0 - byte)[:, None, :]).reshape(k, n).astype(np.float32)
    by_word = np.ascontiguousarray(scaled.reshape(k // 512, 128, 4, n).transpose(0, 1, 3, 2))
    if fmt == "e4m3":
        words = by_word.astype(ml_dtypes.float8_e4m3fn).view(np.uint8)
    else:
        c = by_word.astype(ml_dtypes.float4_e2m1fn).view(np.uint8) & 0xF
        words = (c[..., 0::2] | (c[..., 1::2] << 4)).reshape(k // 512, 128, 2 * n)
    return np.ascontiguousarray(words), np.ascontiguousarray(byte.astype(np.uint8).reshape(k // 512, 16, n))


def unpack_weight(words, scales, fmt):
    g, _, n = scales.shape
    words = np.ascontiguousarray(words).reshape(g, 128, n, -1)
    if fmt == "e4m3":
        vals = words.view(ml_dtypes.float8_e4m3fn).astype(np.float64)
    else:
        nib = np.empty((g, 128, n, 4), np.uint8)
        nib[..., 0::2] = words & 0xF
        nib[..., 1::2] = words >> 4
        vals = E2M1[nib]
    vals = vals * np.repeat(np.exp2(scales.astype(np.float64) - 127.0), 8, axis=1)[..., None]
    return vals.transpose(0, 1, 3, 2).reshape(g * 512, n)


def relu2(v):
    return np.maximum(v, 0.0) ** 2


K, T, E, C, N = 512, 640, 2, 256, 128


def by_expert(wq, xq):
    return np.concatenate([wq[e].T @ xq[:, e * C:(e + 1) * C] for e in range(E)], axis=1)


def setup_inputs():
    n = np.random.standard_normal
    s = mx_kscale(K)[:, None]
    w = [pack_weight(m, "e2m1") for m in n((E, K, N)) / np.sqrt(K) / s[None]]
    return {
        "xT": (n((K, T)) * s).astype(np.float32),
        "xr": n((N, T)).astype(np.float32),
        "w_words": np.stack([m[0] for m in w]),
        "w_scales": np.stack([m[1] for m in w]),
        "b": (0.3 * n((N, E))).astype(np.float32),
        "gate": np.tile(np.random.uniform(0.2, 1.0, E * C), (N, 1)).astype(np.float32),
        "offs": striped(np.random.permutation(T)[:E * C]),
    }


def reference(xT, xr, w_words, w_scales, b, gate, offs):
    idx = unstriped(offs)
    w = np.stack([unpack_weight(w_words[e], w_scales[e], "e2m1") for e in range(E)])
    xq = mxq(f64(xT)[:, idx], 0, "e4m3")
    y = by_expert(w, xq)
    y = relu2(y + np.repeat(f64(b), C, axis=1))
    out = f64(xr).copy()
    out[:, idx] += f64(gate) * y
    return out

@@ -1,0 +1,112 @@
+from contextlib import ExitStack
+
+import concourse.mybir as mybir
+
+K, T, E, C, N = 512, 640, 2, 256, 128
+FLOPS = 2 * K * N * E * C
+
+P = 128
+J = 4
+F32 = mybir.dt.float32
+BF16 = mybir.dt.bfloat16
+I32 = mybir.dt.int32
+U32 = mybir.dt.uint32
+U16 = mybir.dt.uint16
+U8 = mybir.dt.uint8
+FP8X4 = mybir.dt.float8_e4m3fn_x4
+FP4X4 = mybir.dt.float4_e2m1fn_x4
+
+ACT = mybir.ActivationFunctionType
+ALU = mybir.AluOpType
+
+CHUNKS = ((0, 256, 256), (256, 256, 160), (512, 128, 64))
+PIECES = ((0, 384), (384, 256))
+
+
+def tile_moe_res_lin_relu2_kernel(tc, xT, xr, w_words, w_scales, b, gate, offs, out):
+    nc = tc.nc
+    with ExitStack() as ctx:
+        keep = ctx.enter_context(tc.tile_pool(name="keep", bufs=1))
+        psum = ctx.enter_context(tc.psum_pool(name="psum", bufs=1))
+
+        offsets = keep.tile([P, E * C // 16], U16, name="offsets")
+        raws = []
+        groups = []
+        for i, (t0, n, nv) in enumerate(CHUNKS):
+            raws.append(keep.tile([P, J, n], F32, name=f"raw{i}"))
+            groups.append(keep.tile([P, n, J], BF16, align_bytes=64, name=f"group{i}"))
+        codes = keep.tile([P, T], U32, align_bytes=64, name="codes")
+        scales = keep.tile([P, T], U8, align_bytes=64, name="scales")
+        ww = keep.tile([P, E, 2 * N], U8, align_bytes=64, name="ww")
+        ws = keep.tile([P, E, N], U8, align_bytes=64, name="ws")
+        bias = keep.tile([P, E], F32, name="bias")
+        gates = keep.tile([P, E * C], F32, name="gates")
+        resid = keep.tile([P, T], F32, name="resid")
+        window = keep.tile([P, T], F32, name="window")
+        warm = keep.tile([P, 2], F32, name="warm")
+
+        nc.vector.memset(ws[:].rearrange("p e n -> p (e n)").bitcast(I32), 0)
+        nc.vector.memset(warm[:], 0.0)
+        nc.gpsimd.memset(scales[:], 0)
+        nc.gpsimd.memset(window[:], 0.0)
+        x_rows = xT.rearrange("(p j) t -> p j t", j=J)
+        for i, (t0, n, nv) in enumerate(CHUNKS):
+            nc.sync.dma_start(out=raws[i][:], in_=x_rows[:, :, t0 : t0 + n])
+        nc.sync.dma_start(offsets[:], offs)
+        nc.sync.dma_start(out=ww[:].bitcast(I32), in_=w_words.rearrange("e a p c -> p (e a) c").bitcast(I32))
+        for r in range(4):
+            nc.scalar.dma_start(
+                out=ws[r:P:32, :, :].bitcast(I32),
+                in_=w_scales.rearrange("e a (q r) n -> r q (e a) n", r=4)[r].bitcast(I32),
+            )
+        nc.scalar.dma_start(out=bias[:], in_=b)
+        nc.sync.dma_start(out=gates[:], in_=gate)
+        nc.sync.dma_start(out=resid[:], in_=xr)
+        nc.scalar.activation(warm[:, 0:1], warm[:, 1:2], ACT.Relu)
+
+        for i, (t0, n, nv) in enumerate(CHUNKS):
+            nc.vector.tensor_copy(groups[i][:, 0:nv, :], raws[i][:, :, 0:nv].rearrange("p j t -> p t j"))
+            if nv < n:
+                nc.scalar.activation(groups[i][:, nv:n, :], raws[i][:, :, nv:n].rearrange("p j t -> p t j"), ACT.Copy)
+            nc.vector.quantize_mx(
+                out=codes[:, t0 : t0 + n].bitcast(FP8X4),
+                scales=scales[:, t0 : t0 + n],
+                in_=groups[i][:].rearrange("p t j -> p (t j)"),
+            )
+
+        squares = []
+        for e in range(E):
+            cols = offsets[:, e * C // 16 : (e + 1) * C // 16]
+            slot_codes = keep.tile([P, C], U32, align_bytes=64, name=f"slot_codes{e}")
+            slot_scales = keep.tile([P, C], U8, align_bytes=64, name=f"slot_scales{e}")
+            nc.vector.tensor_copy(slot_codes[:], codes[:].indirect(cols))
+            nc.vector.tensor_copy(slot_scales[:], scales[:].indirect(cols))
+            acc = psum.tile([N, C], F32, name=f"acc{e}")
+            nc.tensor.matmul_mx(
+                out=acc[:],
+                lhsT=ww[:, e, :].bitcast(FP4X4),
+                lhsT_scale=ws[:, e, :],
+                rhs=slot_codes[:].bitcast(FP8X4),
+                rhs_scale=slot_scales[:],
+                start=True,
+                stop=True,
+            )
+            relu = keep.tile([N, C], F32, name=f"relu{e}")
+            square = keep.tile([N, C], F32, name=f"square{e}")
+            nc.scalar.activation(relu[:], acc[:], ACT.Relu, bias=bias[:, e : e + 1])
+            nc.scalar.activation(square[:], relu[:], ACT.Square)
+            squares.append(square)
+
+        for e in range(E):
+            nc.vector.tensor_tensor(
+                window[:].indirect(offsets[:, e * C // 16 : (e + 1) * C // 16]),
+                squares[e][:],
+                gates[:, e * C : (e + 1) * C],
+                ALU.mult,
+            )
+
+        for i, (t0, n) in enumerate(PIECES):
+            result = keep.tile([N, n], F32, name=f"result{i}")
+            nc.vector.tensor_tensor(result[:], window[:, t0 : t0 + n], resid[:, t0 : t0 + n], ALU.add)
+            queue = nc.scalar if i else nc.sync
+            queue.dma_start(out=out[:, t0 : t0 + n], in_=result[:])

@@ -19,7 +19,7 @@ FP4X4 = mybir.dt.float4_e2m1fn_x4
 ACT = mybir.ActivationFunctionType
 ALU = mybir.AluOpType
 
-CHUNKS = ((0, 256, 256), (256, 256, 160), (512, 128, 64))
+CHUNKS = ((0, 256, 256), (256, 256, 160), (512, 128, 88))
 PIECES = ((0, 384), (384, 256))
 
 
@@ -43,6 +43,7 @@ def tile_moe_res_lin_relu2_kernel(tc, xT, xr, w_words, w_scales, b, gate, offs, 
         gates = keep.tile([P, E * C], F32, name="gates")
         resid = keep.tile([P, T], F32, name="resid")
         window = keep.tile([P, T], F32, name="window")
+        relu = keep.tile([N, C], F32, name="relu")
         warm = keep.tile([P, 2], F32, name="warm")
 
         nc.vector.memset(ws[:].rearrange("p e n -> p (e n)").bitcast(I32), 0)
@@ -54,13 +55,13 @@ def tile_moe_res_lin_relu2_kernel(tc, xT, xr, w_words, w_scales, b, gate, offs, 
             nc.sync.dma_start(out=raws[i][:], in_=x_rows[:, :, t0 : t0 + n])
         nc.sync.dma_start(offsets[:], offs)
         nc.sync.dma_start(out=ww[:].bitcast(I32), in_=w_words.rearrange("e a p c -> p (e a) c").bitcast(I32))
+        nc.sync.dma_start(out=gates[:], in_=gate)
         for r in range(4):
-            nc.scalar.dma_start(
+            nc.sync.dma_start(
                 out=ws[r:P:32, :, :].bitcast(I32),
                 in_=w_scales.rearrange("e a (q r) n -> r q (e a) n", r=4)[r].bitcast(I32),
             )
-        nc.scalar.dma_start(out=bias[:], in_=b)
-        nc.sync.dma_start(out=gates[:], in_=gate)
+        nc.sync.dma_start(out=bias[:], in_=b)
         nc.sync.dma_start(out=resid[:], in_=xr)
         nc.scalar.activation(warm[:, 0:1], warm[:, 1:2], ACT.Relu)
 
@@ -74,13 +75,15 @@ def tile_moe_res_lin_relu2_kernel(tc, xT, xr, w_words, w_scales, b, gate, offs, 
                 in_=groups[i][:].rearrange("p t j -> p (t j)"),
             )
 
-        squares = []
-        for e in range(E):
+        def gather(e):
             cols = offsets[:, e * C // 16 : (e + 1) * C // 16]
             slot_codes = keep.tile([P, C], U32, align_bytes=64, name=f"slot_codes{e}")
             slot_scales = keep.tile([P, C], U8, align_bytes=64, name=f"slot_scales{e}")
             nc.vector.tensor_copy(slot_codes[:], codes[:].indirect(cols))
             nc.vector.tensor_copy(slot_scales[:], scales[:].indirect(cols))
+            return slot_codes, slot_scales
+
+        def expert(e, slot_codes, slot_scales):
             acc = psum.tile([N, C], F32, name=f"acc{e}")
             nc.tensor.matmul_mx(
                 out=acc[:],
@@ -91,19 +94,23 @@ def tile_moe_res_lin_relu2_kernel(tc, xT, xr, w_words, w_scales, b, gate, offs, 
                 start=True,
                 stop=True,
             )
-            relu = keep.tile([N, C], F32, name=f"relu{e}")
             square = keep.tile([N, C], F32, name=f"square{e}")
             nc.scalar.activation(relu[:], acc[:], ACT.Relu, bias=bias[:, e : e + 1])
             nc.scalar.activation(square[:], relu[:], ACT.Square)
-            squares.append(square)
+            return square
 
-        for e in range(E):
+        def scatter(e, square):
             nc.vector.tensor_tensor(
                 window[:].indirect(offsets[:, e * C // 16 : (e + 1) * C // 16]),
-                squares[e][:],
+                square[:],
                 gates[:, e * C : (e + 1) * C],
                 ALU.mult,
             )
+
+        square0 = expert(0, *gather(0))
+        slots1 = gather(1)
+        scatter(0, square0)
+        scatter(1, expert(1, *slots1))
 
         for i, (t0, n) in enumerate(PIECES):
             result = keep.tile([N, n], F32, name=f"result{i}")

@@ -1,6 +1,7 @@
 from contextlib import ExitStack
 
 import concourse.mybir as mybir
+from concourse.masks import make_identity
 
 K, T, E, C, N = 512, 640, 2, 256, 128
 FLOPS = 2 * K * N * E * C
@@ -20,7 +21,8 @@ ACT = mybir.ActivationFunctionType
 ALU = mybir.AluOpType
 
 CHUNKS = ((0, 256, 256), (256, 256, 160), (512, 128, 88))
-PIECES = ((0, 384), (384, 256))
+PIECES = ((0, 256), (256, 128), (384, 256))
+FLIPPED = 384
 
 
 def tile_moe_res_lin_relu2_kernel(tc, xT, xr, w_words, w_scales, b, gate, offs, out):
@@ -44,12 +46,17 @@ def tile_moe_res_lin_relu2_kernel(tc, xT, xr, w_words, w_scales, b, gate, offs, 
         resid = keep.tile([P, T], F32, name="resid")
         window = keep.tile([P, T], F32, name="window")
         relu = keep.tile([N, C], F32, name="relu")
+        identity = keep.tile([P, P], F32, name="identity")
+        flip = keep.tile([P, FLIPPED], F32, name="flip")
+        bank = psum.tile([N, E * C], F32, name="bank")
+        resid_bank = psum.tile([N, FLIPPED], F32, name="resid_bank")
         warm = keep.tile([P, 2], F32, name="warm")
 
         nc.vector.memset(ws[:].rearrange("p e n -> p (e n)").bitcast(I32), 0)
         nc.vector.memset(warm[:], 0.0)
         nc.gpsimd.memset(scales[:], 0)
         nc.gpsimd.memset(window[:], 0.0)
+        make_identity(nc, identity[:])
         x_rows = xT.rearrange("(p j) t -> p j t", j=J)
         for i, (t0, n, nv) in enumerate(CHUNKS):
             nc.sync.dma_start(out=raws[i][:], in_=x_rows[:, :, t0 : t0 + n])
@@ -84,9 +91,9 @@ def tile_moe_res_lin_relu2_kernel(tc, xT, xr, w_words, w_scales, b, gate, offs, 
             return slot_codes, slot_scales
 
         def expert(e, slot_codes, slot_scales):
-            acc = psum.tile([N, C], F32, name=f"acc{e}")
+            acc = bank[:, e * C : (e + 1) * C]
             nc.tensor.matmul_mx(
-                out=acc[:],
+                out=acc,
                 lhsT=ww[:, e, :].bitcast(FP4X4),
                 lhsT_scale=ws[:, e, :],
                 rhs=slot_codes[:].bitcast(FP8X4),
@@ -95,8 +102,11 @@ def tile_moe_res_lin_relu2_kernel(tc, xT, xr, w_words, w_scales, b, gate, offs, 
                 stop=True,
             )
             square = keep.tile([N, C], F32, name=f"square{e}")
-            nc.scalar.activation(relu[:], acc[:], ACT.Relu, bias=bias[:, e : e + 1])
-            nc.scalar.activation(square[:], relu[:], ACT.Square)
+            half = C // 2 if e == 0 else C
+            for h in range(0, C, half):
+                nc.scalar.activation(relu[:, h : h + half], acc[:, h : h + half], ACT.Relu, bias=bias[:, e : e + 1])
+            for h in range(0, C, half):
+                nc.scalar.activation(square[:, h : h + half], relu[:, h : h + half], ACT.Square)
             return square
 
         def scatter(e, square):
@@ -112,8 +122,17 @@ def tile_moe_res_lin_relu2_kernel(tc, xT, xr, w_words, w_scales, b, gate, offs, 
         scatter(0, square0)
         scatter(1, expert(1, *slots1))
 
+        for i in range(FLIPPED // P):
+            nc.tensor.transpose(bank[:, i * P : (i + 1) * P], resid[:, i * P : (i + 1) * P], identity[:])
+        nc.scalar.copy(flip[:], bank[:, 0:FLIPPED])
+        for i in range(FLIPPED // P):
+            nc.tensor.transpose(resid_bank[:, i * P : (i + 1) * P], flip[:, i * P : (i + 1) * P], identity[:])
+
         for i, (t0, n) in enumerate(PIECES):
             result = keep.tile([N, n], F32, name=f"result{i}")
-            nc.vector.tensor_tensor(result[:], window[:, t0 : t0 + n], resid[:, t0 : t0 + n], ALU.add)
-            queue = nc.scalar if i else nc.sync
+            if i < 2:
+                nc.vector.tensor_tensor(result[:], resid_bank[:, t0 : t0 + n], window[:, t0 : t0 + n], ALU.add)
+            else:
+                nc.gpsimd.tensor_tensor(result[:], resid[:, t0 : t0 + n], window[:, t0 : t0 + n], ALU.add)
+            queue = nc.scalar if i == 2 else nc.sync
             queue.dma_start(out=out[:, t0 : t0 + n], in_=result[:])

from contextlib import ExitStack

import concourse.mybir as mybir
from concourse.masks import make_identity

K, T, E, C, N = 512, 640, 2, 256, 128
FLOPS = 2 * K * N * E * C

P = 128
J = 4
F32 = mybir.dt.float32
BF16 = mybir.dt.bfloat16
I32 = mybir.dt.int32
U32 = mybir.dt.uint32
U16 = mybir.dt.uint16
U8 = mybir.dt.uint8
FP8X4 = mybir.dt.float8_e4m3fn_x4
FP4X4 = mybir.dt.float4_e2m1fn_x4

ACT = mybir.ActivationFunctionType
ALU = mybir.AluOpType

CHUNKS = ((0, 256, 256), (256, 256, 160), (512, 128, 88))
PIECES = ((0, 256), (256, 128), (384, 256))
FLIPPED = 384


def tile_moe_res_lin_relu2_kernel(tc, xT, xr, w_words, w_scales, b, gate, offs, out):
    nc = tc.nc
    with ExitStack() as ctx:
        keep = ctx.enter_context(tc.tile_pool(name="keep", bufs=1))
        psum = ctx.enter_context(tc.psum_pool(name="psum", bufs=1))

        offsets = keep.tile([P, E * C // 16], U16, name="offsets")
        raws = []
        groups = []
        for i, (t0, n, nv) in enumerate(CHUNKS):
            raws.append(keep.tile([P, J, n], F32, name=f"raw{i}"))
            groups.append(keep.tile([P, n, J], BF16, align_bytes=64, name=f"group{i}"))
        codes = keep.tile([P, T], U32, align_bytes=64, name="codes")
        scales = keep.tile([P, T], U8, align_bytes=64, name="scales")
        ww = keep.tile([P, E, 2 * N], U8, align_bytes=64, name="ww")
        ws = keep.tile([P, E, N], U8, align_bytes=64, name="ws")
        bias = keep.tile([P, E], F32, name="bias")
        gates = keep.tile([P, E * C], F32, name="gates")
        resid = keep.tile([P, T], F32, name="resid")
        window = keep.tile([P, T], F32, name="window")
        relu = keep.tile([N, C], F32, name="relu")
        identity = keep.tile([P, P], F32, name="identity")
        flip = keep.tile([P, FLIPPED], F32, name="flip")
        bank = psum.tile([N, E * C], F32, name="bank")
        resid_bank = psum.tile([N, FLIPPED], F32, name="resid_bank")
        warm = keep.tile([P, 2], F32, name="warm")

        nc.vector.memset(ws[:].rearrange("p e n -> p (e n)").bitcast(I32), 0)
        nc.vector.memset(warm[:], 0.0)
        nc.gpsimd.memset(scales[:], 0)
        nc.gpsimd.memset(window[:], 0.0)
        make_identity(nc, identity[:])
        x_rows = xT.rearrange("(p j) t -> p j t", j=J)
        for i, (t0, n, nv) in enumerate(CHUNKS):
            nc.sync.dma_start(out=raws[i][:], in_=x_rows[:, :, t0 : t0 + n])
        nc.sync.dma_start(offsets[:], offs)
        nc.sync.dma_start(out=ww[:].bitcast(I32), in_=w_words.rearrange("e a p c -> p (e a) c").bitcast(I32))
        nc.sync.dma_start(out=gates[:], in_=gate)
        for r in range(4):
            nc.sync.dma_start(
                out=ws[r:P:32, :, :].bitcast(I32),
                in_=w_scales.rearrange("e a (q r) n -> r q (e a) n", r=4)[r].bitcast(I32),
            )
        nc.sync.dma_start(out=bias[:], in_=b)
        nc.sync.dma_start(out=resid[:], in_=xr)
        nc.scalar.activation(warm[:, 0:1], warm[:, 1:2], ACT.Relu)

        for i, (t0, n, nv) in enumerate(CHUNKS):
            nc.vector.tensor_copy(groups[i][:, 0:nv, :], raws[i][:, :, 0:nv].rearrange("p j t -> p t j"))
            if nv < n:
                nc.scalar.activation(groups[i][:, nv:n, :], raws[i][:, :, nv:n].rearrange("p j t -> p t j"), ACT.Copy)
            nc.vector.quantize_mx(
                out=codes[:, t0 : t0 + n].bitcast(FP8X4),
                scales=scales[:, t0 : t0 + n],
                in_=groups[i][:].rearrange("p t j -> p (t j)"),
            )

        def gather(e):
            cols = offsets[:, e * C // 16 : (e + 1) * C // 16]
            slot_codes = keep.tile([P, C], U32, align_bytes=64, name=f"slot_codes{e}")
            slot_scales = keep.tile([P, C], U8, align_bytes=64, name=f"slot_scales{e}")
            nc.vector.tensor_copy(slot_codes[:], codes[:].indirect(cols))
            nc.vector.tensor_copy(slot_scales[:], scales[:].indirect(cols))
            return slot_codes, slot_scales

        def expert(e, slot_codes, slot_scales):
            acc = bank[:, e * C : (e + 1) * C]
            nc.tensor.matmul_mx(
                out=acc,
                lhsT=ww[:, e, :].bitcast(FP4X4),
                lhsT_scale=ws[:, e, :],
                rhs=slot_codes[:].bitcast(FP8X4),
                rhs_scale=slot_scales[:],
                start=True,
                stop=True,
            )
            square = keep.tile([N, C], F32, name=f"square{e}")
            half = C // 2 if e == 0 else C
            for h in range(0, C, half):
                nc.scalar.activation(relu[:, h : h + half], acc[:, h : h + half], ACT.Relu, bias=bias[:, e : e + 1])
            for h in range(0, C, half):
                nc.scalar.activation(square[:, h : h + half], relu[:, h : h + half], ACT.Square)
            return square

        def scatter(e, square):
            nc.vector.tensor_tensor(
                window[:].indirect(offsets[:, e * C // 16 : (e + 1) * C // 16]),
                square[:],
                gates[:, e * C : (e + 1) * C],
                ALU.mult,
            )

        square0 = expert(0, *gather(0))
        slots1 = gather(1)
        scatter(0, square0)
        scatter(1, expert(1, *slots1))

        for i in range(FLIPPED // P):
            nc.tensor.transpose(bank[:, i * P : (i + 1) * P], resid[:, i * P : (i + 1) * P], identity[:])
        nc.scalar.copy(flip[:], bank[:, 0:FLIPPED])
        for i in range(FLIPPED // P):
            nc.tensor.transpose(resid_bank[:, i * P : (i + 1) * P], flip[:, i * P : (i + 1) * P], identity[:])

        for i, (t0, n) in enumerate(PIECES):
            result = keep.tile([N, n], F32, name=f"result{i}")
            if i < 2:
                nc.vector.tensor_tensor(result[:], resid_bank[:, t0 : t0 + n], window[:, t0 : t0 + n], ALU.add)
            else:
                nc.gpsimd.tensor_tensor(result[:], resid[:, t0 : t0 + n], window[:, t0 : t0 + n], ALU.add)
            queue = nc.scalar if i == 2 else nc.sync
            queue.dma_start(out=out[:, t0 : t0 + n], in_=result[:])
